import numpy as np
import ml_dtypes


def mxq(x, axis, fmt="e4m3"):
    dtype, down = {"e4m3": (ml_dtypes.float8_e4m3fn, 7), "e5m2": (ml_dtypes.float8_e5m2, 14)}[fmt]
    v = np.moveaxis(np.asarray(x, np.float32).astype(ml_dtypes.bfloat16).astype(np.float64), axis, -1)
    blocks = v.reshape(v.shape[:-1] + (-1, 32))
    amax = np.abs(blocks).max(-1, keepdims=True)
    byte = np.maximum(np.where(amax > 0, np.frexp(amax)[1] - 1 + 127, 0) - down, 1)
    scale = np.exp2(byte - 127.0)
    codes = (blocks / scale).astype(np.float32).astype(dtype).astype(np.float64)
    return np.moveaxis((codes * scale).reshape(v.shape), -1, axis)


WIDE = False


def mx_kscale(k):
    if not WIDE:
        return np.ones(k)
    levels = np.array([10, -10, 5, -5, 0])
    if k % 512:
        return np.exp2(np.random.permutation(np.resize(levels, k // 32))).repeat(32)
    a = np.empty((k // 512, 16))
    for p in range(k // 512):
        a[p, :8] = np.random.permutation(np.resize(levels, 8))
        for g in range(8):
            far = levels[np.abs(levels - a[p, g]) >= 10]
            a[p, g + 8] = far[np.random.randint(len(far))]
    return np.exp2(a.ravel()).repeat(32)


def f64(x):
    return np.asarray(x).astype(np.float64)


def striped(idx):
    return np.tile(idx.reshape(-1, 16).T, (8, 1)).astype(np.uint16)


def unstriped(offs):
    return offs[:16].T.reshape(-1).astype(np.int64)


E2M1 = np.array([0.0, 0.5, 1.0, 1.5, 2.0, 3.0, 4.0, 6.0, -0.0, -0.5, -1.0, -1.5, -2.0, -3.0, -4.0, -6.0])


def pack_weight(w, fmt):
    k, n = w.shape
    w = f64(np.asarray(w, np.float32).astype(ml_dtypes.bfloat16)).reshape(k // 32, 32, n)
    amax = np.abs(w).max(1)
    if fmt == "e4m3":
        byte = np.frexp(amax)[1] - 1 + 127 - 7
    else:
        mant, ex = np.frexp(amax / 6.0)
        byte = np.where(mant > 0.5, ex, ex - 1) + 127
    byte = np.clip(np.where(amax > 0, byte, 1), 1, 254)
    scaled = (w * np.exp2(127.0 - byte)[:, None, :]).reshape(k, n).astype(np.float32)
    by_word = np.ascontiguousarray(scaled.reshape(k // 512, 128, 4, n).transpose(0, 1, 3, 2))
    if fmt == "e4m3":
        words = by_word.astype(ml_dtypes.float8_e4m3fn).view(np.uint8)
    else:
        c = by_word.astype(ml_dtypes.float4_e2m1fn).view(np.uint8) & 0xF
        words = (c[..., 0::2] | (c[..., 1::2] << 4)).reshape(k // 512, 128, 2 * n)
    return np.ascontiguousarray(words), np.ascontiguousarray(byte.astype(np.uint8).reshape(k // 512, 16, n))


def unpack_weight(words, scales, fmt):
    g, _, n = scales.shape
    words = np.ascontiguousarray(words).reshape(g, 128, n, -1)
    if fmt == "e4m3":
        vals = words.view(ml_dtypes.float8_e4m3fn).astype(np.float64)
    else:
        nib = np.empty((g, 128, n, 4), np.uint8)
        nib[..., 0::2] = words & 0xF
        nib[..., 1::2] = words >> 4
        vals = E2M1[nib]
    vals = vals * np.repeat(np.exp2(scales.astype(np.float64) - 127.0), 8, axis=1)[..., None]
    return vals.transpose(0, 1, 3, 2).reshape(g * 512, n)


def gelu(v):
    return 0.5 * v * (1.0 + np.tanh(np.sqrt(2.0 / np.pi) * (v + 0.044715 * v**3)))


K, T, S, S2 = 1024, 2048, 512, 1024

def setup_inputs():
    n = np.random.standard_normal
    s = mx_kscale(K)[:, None]
    d = {}
    d["tab_words"], d["tab_scales"] = pack_weight(n((K, T)) * s, "e4m3")
    d["offs"] = striped(np.random.permutation(T)[:S])
    d["offs2"] = striped(np.random.permutation(T)[:S2])
    d["w1"] = (n((K, K)) / K / s / s.T).astype(np.float32)
    d["w4_words"], d["w4_scales"] = pack_weight(1.4 * n((K, K)) / K / s / s.T, "e2m1")
    d["th"] = np.random.uniform(0.3, 1.2, S2).astype(np.float32)
    return d

def reference(tab_words, tab_scales, offs, offs2, w1, w4_words, w4_scales, th):
    TW = unpack_weight(tab_words, tab_scales, "e4m3")
    v = TW[:, unstriped(offs)]
    v2 = TW[:, unstriped(offs2)]
    w1q = mxq(f64(w1), 0, "e4m3")
    w4 = unpack_weight(w4_words, w4_scales, "e2m1")
    h1 = np.abs(w1q.T @ v)
    h2 = np.maximum(w4.T @ v, 0.0)
    e1 = v2.T @ mxq(h1, 0, "e4m3")
    e2 = v2.T @ mxq(h2, 0, "e4m3")
    link = np.minimum(e1, e2)
    out = link - f64(th)[:, None]
    return out

@@ -1,0 +1,233 @@
+from contextlib import ExitStack
+
+import concourse.mybir as mybir
+from concourse.masks import make_identity
+
+K, T, S, S2 = 1024, 2048, 512, 1024
+FLOPS = 2 * (2 * K * K * S + 2 * K * S2 * S)
+
+F32 = mybir.dt.float32
+BF16 = mybir.dt.bfloat16
+I32 = mybir.dt.int32
+U32 = mybir.dt.uint32
+U16 = mybir.dt.uint16
+U8 = mybir.dt.uint8
+FP8X4 = mybir.dt.float8_e4m3fn_x4
+FP4X4 = mybir.dt.float4_e2m1fn_x4
+ACT = mybir.ActivationFunctionType
+ALU = mybir.AluOpType
+
+P = 128
+PACK = 4
+PASS = P * PACK
+PASSES = K // PASS
+BANK = 512
+QUADS = 4
+SCALAR_M = {(0, 0): 0, (1, 0): 32, (0, 1): 48, (1, 1): 48}
+
+
+def tile_list_print_link_scores_kernel(
+    tc, tab_words, tab_scales, offs, offs2, w1, w4_words, w4_scales, th, out
+):
+    nc = tc.nc
+    with ExitStack() as ctx:
+        keep = ctx.enter_context(tc.tile_pool(name="keep", bufs=1))
+        ring = ctx.enter_context(tc.tile_pool(name="ring", bufs=4))
+        psum = ctx.enter_context(tc.psum_pool(name="psum", bufs=8))
+
+        def held(name, shape, dtype):
+            return keep.tile(shape, dtype, name=name, align_bytes=64)
+
+        idx = held("idx", [P, S // 16], U16)
+        idx2 = held("idx2", [P, S2 // 16], U16)
+        tab_s01 = held("tab_s01", [P, T], U8)
+        tab_s1 = held("tab_s1", [P, T], U8)
+        w4_s = held("w4_s", [P, PASSES * K], U8)
+        tab_w = [held("tab_w%d" % a, [P, T], I32) for a in range(PASSES)]
+        w4_w = [held("w4_w%d" % a, [P, 2 * K], U8) for a in range(PASSES)]
+        th_rows = held("th_rows", [P, P], F32)
+        neg_th = held("neg_th", [P, S2 // P], F32)
+        ident = held("ident", [P, P], F32)
+
+        nc.vector.memset(tab_s01[:].bitcast(I32), 0)
+        nc.gpsimd.memset(tab_s1[:].bitcast(I32), 0)
+        nc.vector.memset(w4_s[:].bitcast(I32), 0)
+        nc.vector.memset(th_rows[:], 0.0)
+
+        nc.sync.dma_start(idx[:], offs)
+        nc.sync.dma_start(idx2[:], offs2)
+        for q in range(QUADS):
+            nc.sync.dma_start(
+                tab_s01[32 * q : 32 * q + 8, :].bitcast(I32),
+                tab_scales[:, 4 * q : 4 * q + 4, :].bitcast(I32),
+            )
+        for q in range(QUADS):
+            nc.gpsimd.dma_start(
+                tab_s1[32 * q : 32 * q + 4, :].bitcast(I32),
+                tab_scales[1, 4 * q : 4 * q + 4, :].bitcast(I32),
+            )
+        nc.gpsimd.dma_start(th_rows[: S2 // P, :], th.rearrange("(c p) -> c p", p=P))
+        for a in range(PASSES):
+            nc.sync.dma_start(tab_w[a][:], tab_words[a].rearrange("p t i -> p (t i)").bitcast(I32))
+            nc.sync.dma_start(w4_w[a][:].bitcast(I32), w4_words[a].bitcast(I32))
+            if a == 0:
+                for q in range(QUADS):
+                    nc.sync.dma_start(
+                        w4_s[32 * q : 32 * q + 4, :].bitcast(I32).rearrange("r (a c) -> r a c", a=PASSES),
+                        w4_scales[:, 4 * q : 4 * q + 4, :].bitcast(I32).rearrange("a r c -> r a c"),
+                    )
+        w1_raw = {}
+        for b in range(PASSES):
+            for a in range(PASSES):
+                w1_raw[a, b] = held("w1_raw%d%d" % (a, b), [P, PACK, PASS], F32)
+                nc.sync.dma_start(
+                    w1_raw[a, b][:],
+                    w1[a * PASS : (a + 1) * PASS, b * PASS : (b + 1) * PASS].rearrange("(p j) c -> p j c", j=PACK),
+                )
+        make_identity(nc, ident[:])
+        th_bank = psum.tile([P, BANK], F32, name="bank")
+        nc.tensor.transpose(th_bank[:, :P], th_rows[:], ident[:])
+        nc.scalar.activation(neg_th[:], th_bank[:, : S2 // P], ACT.Identity, scale=-1.0)
+
+        def gather(name, window, offsets, dtype):
+            picked = held(name, [P, 512], dtype)
+            nc.vector.tensor_copy(picked[:], window.indirect(offsets))
+            return picked
+
+        def half2(h):
+            return idx2[:, 32 * h : 32 * (h + 1)]
+
+        v_s = [gather("v_s0", tab_s01[:], idx[:], U8), gather("v_s1", tab_s1[:], idx[:], U8)]
+        v_w = [gather("v_w%d" % a, tab_w[a][:].bitcast(U32), idx[:], U32) for a in range(PASSES)]
+
+        h2_w, h2_s = [], []
+        for b in range(PASSES):
+            grouped = held("h2_g%d" % b, [P, S * PACK], BF16)
+            for pair in range(2):
+                turned = []
+                for jt in (2 * pair, 2 * pair + 1):
+                    acc = psum.tile([P, BANK], F32, name="bank")
+                    for a in range(PASSES):
+                        nc.tensor.matmul_mx(
+                            out=acc[:],
+                            lhsT=v_w[a][:, jt * P : (jt + 1) * P].bitcast(FP8X4),
+                            lhsT_scale=v_s[a][:, jt * P : (jt + 1) * P],
+                            rhs=w4_w[a][:, 2 * b * PASS : 2 * (b + 1) * PASS].bitcast(FP4X4),
+                            rhs_scale=w4_s[:, a * K + b * PASS : a * K + (b + 1) * PASS],
+                            start=(a == 0),
+                            stop=(a == PASSES - 1),
+                        )
+                    h2t = ring.tile([P, BANK], BF16, name="h2t")
+                    nc.scalar.activation(
+                        h2t[:].rearrange("j (u p e) -> j u p e", u=2, e=2),
+                        acc[:].rearrange("j (p u e) -> j u p e", u=2, e=2),
+                        ACT.Relu,
+                    )
+                    turned.append(h2t)
+                back = psum.tile([P, BANK], F32, name="bank")
+                for i in range(2):
+                    for u in range(2):
+                        nc.tensor.transpose(
+                            back[:, (2 * i + u) * P : (2 * i + u + 1) * P],
+                            turned[i][:].bitcast(F32)[:, u * P : (u + 1) * P],
+                            ident[:],
+                        )
+                nc.scalar.copy(
+                    grouped[:].bitcast(F32)[:, pair * BANK : (pair + 1) * BANK].rearrange("p (i j u) -> p i j u", i=2, u=2),
+                    back[:].rearrange("p (i u j) -> p i j u", i=2, u=2),
+                )
+            codes = held("h2_w%d" % b, [P, S], U32)
+            plane = held("h2_s%d" % b, [P, S], U8)
+            nc.vector.quantize_mx(out=codes[:].bitcast(FP8X4), scales=plane[:], in_=grouped[:])
+            h2_w.append(codes)
+            h2_s.append(plane)
+
+        v2_s = [gather("v2_s%d" % h, tab_s01[:], half2(h), U8) for h in range(2)]
+        v2_w = [
+            [gather("v2_w%d%d" % (a, h), tab_w[a][:].bitcast(U32), half2(h), U32) for a in range(PASSES)]
+            for h in range(2)
+        ]
+
+        def quantise_w1(a, b):
+            grouped = held("w1_g%d%d" % (a, b), [P, PASS * PACK], BF16)
+            dst = grouped[:].rearrange("p (t m j) -> p m j t", t=PACK, j=PACK)
+            src = w1_raw[a, b][:].rearrange("p j (m t) -> p m j t", t=PACK)
+            split = SCALAR_M[a, b]
+            if split > 0:
+                nc.scalar.copy(dst[:, :split], src[:, :split])
+            nc.vector.tensor_copy(dst[:, split:], src[:, split:])
+            codes = held("w1_w%d%d" % (a, b), [P, PASS], U32)
+            plane = held("w1_s%d%d" % (a, b), [P, PASS], U8)
+            nc.vector.quantize_mx(out=codes[:].bitcast(FP8X4), scales=plane[:], in_=grouped[:])
+            return codes, plane
+
+        h1_w, h1_s = [], []
+
+        def make_h1(b):
+            w1_q = [quantise_w1(a, b) for a in range(PASSES)]
+            grouped = held("h1_g%d" % b, [P, S * PACK], BF16)
+            codes = held("h1_w%d" % b, [P, S], U32)
+            plane = held("h1_s%d" % b, [P, S], U8)
+            for jt in range(S // P):
+                acc = psum.tile([P, BANK], F32, name="bank")
+                for t in range(PACK):
+                    for a in range(PASSES):
+                        nc.tensor.matmul_mx(
+                            out=acc[:, t * P : (t + 1) * P],
+                            lhsT=w1_q[a][0][:, t * P : (t + 1) * P].bitcast(FP8X4),
+                            lhsT_scale=w1_q[a][1][:, t * P : (t + 1) * P],
+                            rhs=v_w[a][:, jt * P : (jt + 1) * P].bitcast(FP8X4),
+                            rhs_scale=v_s[a][:, jt * P : (jt + 1) * P],
+                            start=(a == 0),
+                            stop=(a == PASSES - 1),
+                        )
+                nc.scalar.activation(
+                    grouped[:, jt * BANK : (jt + 1) * BANK].rearrange("p (n t) -> p n t", t=PACK),
+                    acc[:].rearrange("p (t n) -> p n t", t=PACK),
+                    ACT.Abs,
+                )
+                if jt % 2 == 1:
+                    cols = slice((jt - 1) * P, (jt + 1) * P)
+                    nc.vector.quantize_mx(
+                        out=codes[:, cols].bitcast(FP8X4),
+                        scales=plane[:, cols],
+                        in_=grouped[:, (jt - 1) * BANK : (jt + 1) * BANK],
+                    )
+            h1_w.append(codes)
+            h1_s.append(plane)
+
+        def match(mt, h_w, h_s):
+            h, cols = mt // 4, slice((mt % 4) * P, (mt % 4 + 1) * P)
+            acc = psum.tile([P, BANK], F32, name="bank")
+            for a in range(PASSES):
+                nc.tensor.matmul_mx(
+                    out=acc[:],
+                    lhsT=v2_w[h][a][:, cols].bitcast(FP8X4),
+                    lhsT_scale=v2_s[h][4 * a : P, cols],
+                    rhs=h_w[a][:].bitcast(FP8X4),
+                    rhs_scale=h_s[a][:],
+                    start=(a == 0),
+                    stop=(a == PASSES - 1),
+                )
+            return acc
+
+        e2_less = {}
+
+        def make_e2(mt):
+            acc = match(mt, h2_w, h2_s)
+            e2_less[mt] = held("e2_less%d" % mt, [P, S], F32)
+            nc.scalar.activation(e2_less[mt][:], acc[:], ACT.Identity, bias=neg_th[:, mt : mt + 1])
+
+        make_h1(0)
+        for mt in range(4):
+            make_e2(mt)
+        make_h1(1)
+        for mt in range(4, 8):
+            make_e2(mt)
+        for mt in range(S2 // P):
+            acc = match(mt, h1_w, h1_s)
+            result = ring.tile([P, S], F32, name="result")
+            nc.vector.scalar_tensor_tensor(
+                result[:], acc[:], neg_th[:, mt : mt + 1], e2_less[mt][:], ALU.add, ALU.min
+            )
+            nc.sync.dma_start(out[mt * P : (mt + 1) * P, :], result[:])

@@ -23,7 +23,7 @@ PASS = P * PACK
 PASSES = K // PASS
 BANK = 512
 QUADS = 4
-SCALAR_M = {(0, 0): 0, (1, 0): 32, (0, 1): 48, (1, 1): 48}
+ON_SCALAR = (0, 1)
 
 
 def tile_list_print_link_scores_kernel(
@@ -33,15 +33,15 @@ def tile_list_print_link_scores_kernel(
     with ExitStack() as ctx:
         keep = ctx.enter_context(tc.tile_pool(name="keep", bufs=1))
         ring = ctx.enter_context(tc.tile_pool(name="ring", bufs=4))
-        psum = ctx.enter_context(tc.psum_pool(name="psum", bufs=8))
+        psum = ctx.enter_context(tc.psum_pool(name="psum", bufs=4))
 
-        def held(name, shape, dtype):
-            return keep.tile(shape, dtype, name=name, align_bytes=64)
+        def held(name, shape, dtype, tag=None):
+            return keep.tile(shape, dtype, name=name, tag=tag or name, align_bytes=64)
 
         idx = held("idx", [P, S // 16], U16)
         idx2 = held("idx2", [P, S2 // 16], U16)
         tab_s01 = held("tab_s01", [P, T], U8)
-        tab_s1 = held("tab_s1", [P, T], U8)
+        v_s1 = held("v_s1", [P, S], U8)
         w4_s = held("w4_s", [P, PASSES * K], U8)
         tab_w = [held("tab_w%d" % a, [P, T], I32) for a in range(PASSES)]
         w4_w = [held("w4_w%d" % a, [P, 2 * K], U8) for a in range(PASSES)]
@@ -50,32 +50,40 @@ def tile_list_print_link_scores_kernel(
         ident = held("ident", [P, P], F32)
 
         nc.vector.memset(tab_s01[:].bitcast(I32), 0)
-        nc.gpsimd.memset(tab_s1[:].bitcast(I32), 0)
+        nc.gpsimd.memset(v_s1[:].bitcast(I32), 0)
         nc.vector.memset(w4_s[:].bitcast(I32), 0)
         nc.vector.memset(th_rows[:], 0.0)
 
+        def load_words(a):
+            nc.sync.dma_start(tab_w[a][:], tab_words[a].rearrange("p t i -> p (t i)").bitcast(I32))
+
         nc.sync.dma_start(idx[:], offs)
         nc.sync.dma_start(idx2[:], offs2)
+        nc.sync.dma_start(w4_w[0][:].bitcast(I32), w4_words[0].bitcast(I32))
         for q in range(QUADS):
             nc.sync.dma_start(
                 tab_s01[32 * q : 32 * q + 8, :].bitcast(I32),
                 tab_scales[:, 4 * q : 4 * q + 4, :].bitcast(I32),
             )
+        load_words(0)
         for q in range(QUADS):
-            nc.gpsimd.dma_start(
-                tab_s1[32 * q : 32 * q + 4, :].bitcast(I32),
-                tab_scales[1, 4 * q : 4 * q + 4, :].bitcast(I32),
+            nc.sync.dma_start(
+                w4_s[32 * q : 32 * q + 4, :].bitcast(I32).rearrange("r (a c) -> r a c", a=PASSES),
+                w4_scales[:, 4 * q : 4 * q + 4, :].bitcast(I32).rearrange("a r c -> r a c"),
             )
-        nc.gpsimd.dma_start(th_rows[: S2 // P, :], th.rearrange("(c p) -> c p", p=P))
-        for a in range(PASSES):
-            nc.sync.dma_start(tab_w[a][:], tab_words[a].rearrange("p t i -> p (t i)").bitcast(I32))
-            nc.sync.dma_start(w4_w[a][:].bitcast(I32), w4_words[a].bitcast(I32))
-            if a == 0:
-                for q in range(QUADS):
-                    nc.sync.dma_start(
-                        w4_s[32 * q : 32 * q + 4, :].bitcast(I32).rearrange("r (a c) -> r a c", a=PASSES),
-                        w4_scales[:, 4 * q : 4 * q + 4, :].bitcast(I32).rearrange("a r c -> r a c"),
-                    )
+        load_words(1)
+        nc.sync.dma_start(w4_w[1][:].bitcast(I32), w4_words[1].bitcast(I32))
+
+        def gather(name, window, offsets, dtype, tag=None):
+            picked = held(name, [P, 512], dtype, tag)
+            nc.vector.tensor_copy(picked[:], window.indirect(offsets))
+            return picked
+
+        v_s01 = gather("v_s01", tab_s01[:], idx[:], U8)
+        for q in range(QUADS):
+            nc.sync.dma_start(
+                v_s1[32 * q : 32 * q + 4, :].bitcast(I32), v_s01[32 * q + 4 : 32 * q + 8, :].bitcast(I32)
+            )
         w1_raw = {}
         for b in range(PASSES):
             for a in range(PASSES):
@@ -84,20 +92,13 @@ def tile_list_print_link_scores_kernel(
                     w1_raw[a, b][:],
                     w1[a * PASS : (a + 1) * PASS, b * PASS : (b + 1) * PASS].rearrange("(p j) c -> p j c", j=PACK),
                 )
+        nc.sync.dma_start(th_rows[: S2 // P, :], th.rearrange("(c p) -> c p", p=P))
         make_identity(nc, ident[:])
-        th_bank = psum.tile([P, BANK], F32, name="bank")
-        nc.tensor.transpose(th_bank[:, :P], th_rows[:], ident[:])
-        nc.scalar.activation(neg_th[:], th_bank[:, : S2 // P], ACT.Identity, scale=-1.0)
-
-        def gather(name, window, offsets, dtype):
-            picked = held(name, [P, 512], dtype)
-            nc.vector.tensor_copy(picked[:], window.indirect(offsets))
-            return picked
 
         def half2(h):
             return idx2[:, 32 * h : 32 * (h + 1)]
 
-        v_s = [gather("v_s0", tab_s01[:], idx[:], U8), gather("v_s1", tab_s1[:], idx[:], U8)]
+        v_s = [v_s01, v_s1]
         v_w = [gather("v_w%d" % a, tab_w[a][:].bitcast(U32), idx[:], U32) for a in range(PASSES)]
 
         h2_w, h2_s = [], []
@@ -106,7 +107,7 @@ def tile_list_print_link_scores_kernel(
             for pair in range(2):
                 turned = []
                 for jt in (2 * pair, 2 * pair + 1):
-                    acc = psum.tile([P, BANK], F32, name="bank")
+                    acc = psum.tile([P, BANK], F32, name="right" if (b, pair) == (1, 0) else "left")
                     for a in range(PASSES):
                         nc.tensor.matmul_mx(
                             out=acc[:],
@@ -124,7 +125,7 @@ def tile_list_print_link_scores_kernel(
                         ACT.Relu,
                     )
                     turned.append(h2t)
-                back = psum.tile([P, BANK], F32, name="bank")
+                back = psum.tile([P, BANK], F32, name="right")
                 for i in range(2):
                     for u in range(2):
                         nc.tensor.transpose(
@@ -142,70 +143,73 @@ def tile_list_print_link_scores_kernel(
             h2_w.append(codes)
             h2_s.append(plane)
 
-        v2_s = [gather("v2_s%d" % h, tab_s01[:], half2(h), U8) for h in range(2)]
-        v2_w = [
-            [gather("v2_w%d%d" % (a, h), tab_w[a][:].bitcast(U32), half2(h), U32) for a in range(PASSES)]
-            for h in range(2)
-        ]
+        v2_s, v2_w = {}, {}
+
+        def gather2_scales(h, tag=None):
+            v2_s[h] = gather("v2_s%d" % h, tab_s01[:], half2(h), U8, tag)
+
+        def gather2_words(h, a, tag=None):
+            v2_w[h, a] = gather("v2_w%d%d" % (h, a), tab_w[a][:].bitcast(U32), half2(h), U32, tag)
+
+        w1_g, w1_q = {}, {}
+
+        def round_w1(a, b):
+            w1_g[a, b] = held("w1_g%d%d" % (a, b), [P, PASS * PACK], BF16)
+            dst = w1_g[a, b][:].rearrange("p (t m j) -> p m t j", t=PACK, j=PACK)
+            src = w1_raw[a, b][:].rearrange("p j (m t) -> p m t j", t=PACK)
+            if (a, b) == ON_SCALAR:
+                for half in (slice(0, P // 2), slice(P // 2, P)):
+                    nc.scalar.copy(dst[:, half], src[:, half])
+            else:
+                nc.vector.tensor_copy(dst, src)
 
         def quantise_w1(a, b):
-            grouped = held("w1_g%d%d" % (a, b), [P, PASS * PACK], BF16)
-            dst = grouped[:].rearrange("p (t m j) -> p m j t", t=PACK, j=PACK)
-            src = w1_raw[a, b][:].rearrange("p j (m t) -> p m j t", t=PACK)
-            split = SCALAR_M[a, b]
-            if split > 0:
-                nc.scalar.copy(dst[:, :split], src[:, :split])
-            nc.vector.tensor_copy(dst[:, split:], src[:, split:])
             codes = held("w1_w%d%d" % (a, b), [P, PASS], U32)
             plane = held("w1_s%d%d" % (a, b), [P, PASS], U8)
-            nc.vector.quantize_mx(out=codes[:].bitcast(FP8X4), scales=plane[:], in_=grouped[:])
-            return codes, plane
+            nc.vector.quantize_mx(out=codes[:].bitcast(FP8X4), scales=plane[:], in_=w1_g[a, b][:])
+            w1_q[a, b] = codes, plane
 
         h1_w, h1_s = [], []
 
         def make_h1(b):
-            w1_q = [quantise_w1(a, b) for a in range(PASSES)]
-            grouped = held("h1_g%d" % b, [P, S * PACK], BF16)
             codes = held("h1_w%d" % b, [P, S], U32)
             plane = held("h1_s%d" % b, [P, S], U8)
+            banks = [psum.tile([P, BANK], F32, name="left") for jt in range(S // P)]
             for jt in range(S // P):
-                acc = psum.tile([P, BANK], F32, name="bank")
-                for t in range(PACK):
-                    for a in range(PASSES):
+                for a in range(PASSES):
+                    for t in range(PACK):
                         nc.tensor.matmul_mx(
-                            out=acc[:, t * P : (t + 1) * P],
-                            lhsT=w1_q[a][0][:, t * P : (t + 1) * P].bitcast(FP8X4),
-                            lhsT_scale=w1_q[a][1][:, t * P : (t + 1) * P],
+                            out=banks[jt][:, t * P : (t + 1) * P],
+                            lhsT=w1_q[a, b][0][:, t * P : (t + 1) * P].bitcast(FP8X4),
+                            lhsT_scale=w1_q[a, b][1][:, t * P : (t + 1) * P],
                             rhs=v_w[a][:, jt * P : (jt + 1) * P].bitcast(FP8X4),
                             rhs_scale=v_s[a][:, jt * P : (jt + 1) * P],
-                            start=(a == 0),
-                            stop=(a == PASSES - 1),
+                            start=(a == 0 and t == 0),
+                            stop=(a == PASSES - 1 and t == PACK - 1),
                         )
-                nc.scalar.activation(
-                    grouped[:, jt * BANK : (jt + 1) * BANK].rearrange("p (n t) -> p n t", t=PACK),
-                    acc[:].rearrange("p (t n) -> p n t", t=PACK),
-                    ACT.Abs,
-                )
-                if jt % 2 == 1:
-                    cols = slice((jt - 1) * P, (jt + 1) * P)
-                    nc.vector.quantize_mx(
-                        out=codes[:, cols].bitcast(FP8X4),
-                        scales=plane[:, cols],
-                        in_=grouped[:, (jt - 1) * BANK : (jt + 1) * BANK],
+            for pair in range(2):
+                grouped = held("h1_g%d%d" % (b, pair), [P, 2 * BANK], BF16)
+                for i in range(2):
+                    nc.scalar.activation(
+                        grouped[:, i * BANK : (i + 1) * BANK].rearrange("p (n t) -> p n t", t=PACK),
+                        banks[2 * pair + i][:].rearrange("p (t n) -> p n t", t=PACK),
+                        ACT.Abs,
                     )
+                cols = slice(2 * pair * P, 2 * (pair + 1) * P)
+                nc.vector.quantize_mx(out=codes[:, cols].bitcast(FP8X4), scales=plane[:, cols], in_=grouped[:])
             h1_w.append(codes)
             h1_s.append(plane)
 
-        def match(mt, h_w, h_s):
+        def match(mt, h_w, h_s, side, notes=slice(0, S)):
             h, cols = mt // 4, slice((mt % 4) * P, (mt % 4 + 1) * P)
-            acc = psum.tile([P, BANK], F32, name="bank")
+            acc = psum.tile([P, BANK], F32, name=side)
             for a in range(PASSES):
                 nc.tensor.matmul_mx(
-                    out=acc[:],
-                    lhsT=v2_w[h][a][:, cols].bitcast(FP8X4),
+                    out=acc[:, notes],
+                    lhsT=v2_w[h, a][:, cols].bitcast(FP8X4),
                     lhsT_scale=v2_s[h][4 * a : P, cols],
-                    rhs=h_w[a][:].bitcast(FP8X4),
-                    rhs_scale=h_s[a][:],
+                    rhs=h_w[a][:, notes].bitcast(FP8X4),
+                    rhs_scale=h_s[a][:, notes],
                     start=(a == 0),
                     stop=(a == PASSES - 1),
                 )
@@ -213,21 +217,43 @@ def tile_list_print_link_scores_kernel(
 
         e2_less = {}
 
-        def make_e2(mt):
-            acc = match(mt, h2_w, h2_s)
+        def drain_e2(mt, acc):
             e2_less[mt] = held("e2_less%d" % mt, [P, S], F32)
             nc.scalar.activation(e2_less[mt][:], acc[:], ACT.Identity, bias=neg_th[:, mt : mt + 1])
 
-        make_h1(0)
-        for mt in range(4):
-            make_e2(mt)
-        make_h1(1)
-        for mt in range(4, 8):
-            make_e2(mt)
-        for mt in range(S2 // P):
-            acc = match(mt, h1_w, h1_s)
+        th_bank = psum.tile([P, BANK], F32, name="right")
+        nc.tensor.transpose(th_bank[:, :P], th_rows[:], ident[:])
+        nc.scalar.activation(neg_th[:], th_bank[:, : S2 // P], ACT.Identity, scale=-1.0)
+        def make_out(mt, notes=slice(0, S)):
+            acc = match(mt, h1_w, h1_s, "left", notes)
             result = ring.tile([P, S], F32, name="result")
             nc.vector.scalar_tensor_tensor(
-                result[:], acc[:], neg_th[:, mt : mt + 1], e2_less[mt][:], ALU.add, ALU.min
+                result[:, notes], acc[:, notes], neg_th[:, mt : mt + 1], e2_less[mt][:, notes], ALU.add, ALU.min
             )
-            nc.sync.dma_start(out[mt * P : (mt + 1) * P, :], result[:])
+            nc.sync.dma_start(out[mt * P : (mt + 1) * P, notes], result[:, notes])
+
+        gather2_scales(0)
+        gather2_words(0, 0)
+        gather2_words(0, 1)
+        for a in range(PASSES):
+            round_w1(a, 0)
+            quantise_w1(a, 0)
+        round_w1(0, 1)
+        make_h1(0)
+        round_w1(1, 1)
+        quantise_w1(0, 1)
+        quantise_w1(1, 1)
+        make_h1(1)
+        early = [match(mt, h2_w, h2_s, "right") for mt in range(4)]
+        gather2_scales(1, "w1_g11")
+        gather2_words(1, 0, "w1_g01")
+        gather2_words(1, 1, "h1_g01")
+        for mt in range(4):
+            drain_e2(mt, early[mt])
+            make_out(mt)
+        for mt in range(4, 8):
+            drain_e2(mt, match(mt, h2_w, h2_s, "right"))
+            if mt < 7:
+                make_out(mt)
+        make_out(7, slice(0, S // 2))
+        make_out(7, slice(S // 2, S))

@@ -23,7 +23,7 @@ PASS = P * PACK
 PASSES = K // PASS
 BANK = 512
 QUADS = 4
-ON_SCALAR = (0, 1)
+ON_SCALAR = (1, 1)
 
 
 def tile_list_print_link_scores_kernel(
@@ -226,7 +226,7 @@ def tile_list_print_link_scores_kernel(
         nc.scalar.activation(neg_th[:], th_bank[:, : S2 // P], ACT.Identity, scale=-1.0)
         def make_out(mt, notes=slice(0, S)):
             acc = match(mt, h1_w, h1_s, "left", notes)
-            result = ring.tile([P, S], F32, name="result")
+            result = held("result%d_%d" % (mt, notes.start), [P, S], F32)
             nc.vector.scalar_tensor_tensor(
                 result[:, notes], acc[:, notes], neg_th[:, mt : mt + 1], e2_less[mt][:, notes], ALU.add, ALU.min
             )
@@ -239,20 +239,19 @@ def tile_list_print_link_scores_kernel(
             round_w1(a, 0)
             quantise_w1(a, 0)
         round_w1(0, 1)
-        make_h1(0)
-        round_w1(1, 1)
         quantise_w1(0, 1)
+        round_w1(1, 1)
+        make_h1(0)
+        e2 = [match(mt, h2_w, h2_s, "right") for mt in range(4)]
         quantise_w1(1, 1)
         make_h1(1)
-        early = [match(mt, h2_w, h2_s, "right") for mt in range(4)]
-        gather2_scales(1, "w1_g11")
-        gather2_words(1, 0, "w1_g01")
-        gather2_words(1, 1, "h1_g01")
-        for mt in range(4):
-            drain_e2(mt, early[mt])
-            make_out(mt)
-        for mt in range(4, 8):
-            drain_e2(mt, match(mt, h2_w, h2_s, "right"))
+        gather2_scales(1, "w1_g01")
+        gather2_words(1, 0, "h2_g1")
+        gather2_words(1, 1, "w1_g11")
+        for mt in range(8):
+            drain_e2(mt, e2[mt])
+            if mt < 4:
+                e2.append(match(mt + 4, h2_w, h2_s, "right"))
             if mt < 7:
                 make_out(mt)
         make_out(7, slice(0, S // 2))

from contextlib import ExitStack

import concourse.mybir as mybir
from concourse.masks import make_identity

K, T, S, S2 = 1024, 2048, 512, 1024
FLOPS = 2 * (2 * K * K * S + 2 * K * S2 * S)

F32 = mybir.dt.float32
BF16 = mybir.dt.bfloat16
I32 = mybir.dt.int32
U32 = mybir.dt.uint32
U16 = mybir.dt.uint16
U8 = mybir.dt.uint8
FP8X4 = mybir.dt.float8_e4m3fn_x4
FP4X4 = mybir.dt.float4_e2m1fn_x4
ACT = mybir.ActivationFunctionType
ALU = mybir.AluOpType

P = 128
PACK = 4
PASS = P * PACK
PASSES = K // PASS
BANK = 512
QUADS = 4
ON_SCALAR = (1, 1)


def tile_list_print_link_scores_kernel(
    tc, tab_words, tab_scales, offs, offs2, w1, w4_words, w4_scales, th, out
):
    nc = tc.nc
    with ExitStack() as ctx:
        keep = ctx.enter_context(tc.tile_pool(name="keep", bufs=1))
        ring = ctx.enter_context(tc.tile_pool(name="ring", bufs=4))
        psum = ctx.enter_context(tc.psum_pool(name="psum", bufs=4))

        def held(name, shape, dtype, tag=None):
            return keep.tile(shape, dtype, name=name, tag=tag or name, align_bytes=64)

        idx = held("idx", [P, S // 16], U16)
        idx2 = held("idx2", [P, S2 // 16], U16)
        tab_s01 = held("tab_s01", [P, T], U8)
        v_s1 = held("v_s1", [P, S], U8)
        w4_s = held("w4_s", [P, PASSES * K], U8)
        tab_w = [held("tab_w%d" % a, [P, T], I32) for a in range(PASSES)]
        w4_w = [held("w4_w%d" % a, [P, 2 * K], U8) for a in range(PASSES)]
        th_rows = held("th_rows", [P, P], F32)
        neg_th = held("neg_th", [P, S2 // P], F32)
        ident = held("ident", [P, P], F32)

        nc.vector.memset(tab_s01[:].bitcast(I32), 0)
        nc.gpsimd.memset(v_s1[:].bitcast(I32), 0)
        nc.vector.memset(w4_s[:].bitcast(I32), 0)
        nc.vector.memset(th_rows[:], 0.0)

        def load_words(a):
            nc.sync.dma_start(tab_w[a][:], tab_words[a].rearrange("p t i -> p (t i)").bitcast(I32))

        nc.sync.dma_start(idx[:], offs)
        nc.sync.dma_start(idx2[:], offs2)
        nc.sync.dma_start(w4_w[0][:].bitcast(I32), w4_words[0].bitcast(I32))
        for q in range(QUADS):
            nc.sync.dma_start(
                tab_s01[32 * q : 32 * q + 8, :].bitcast(I32),
                tab_scales[:, 4 * q : 4 * q + 4, :].bitcast(I32),
            )
        load_words(0)
        for q in range(QUADS):
            nc.sync.dma_start(
                w4_s[32 * q : 32 * q + 4, :].bitcast(I32).rearrange("r (a c) -> r a c", a=PASSES),
                w4_scales[:, 4 * q : 4 * q + 4, :].bitcast(I32).rearrange("a r c -> r a c"),
            )
        load_words(1)
        nc.sync.dma_start(w4_w[1][:].bitcast(I32), w4_words[1].bitcast(I32))

        def gather(name, window, offsets, dtype, tag=None):
            picked = held(name, [P, 512], dtype, tag)
            nc.vector.tensor_copy(picked[:], window.indirect(offsets))
            return picked

        v_s01 = gather("v_s01", tab_s01[:], idx[:], U8)
        for q in range(QUADS):
            nc.sync.dma_start(
                v_s1[32 * q : 32 * q + 4, :].bitcast(I32), v_s01[32 * q + 4 : 32 * q + 8, :].bitcast(I32)
            )
        w1_raw = {}
        for b in range(PASSES):
            for a in range(PASSES):
                w1_raw[a, b] = held("w1_raw%d%d" % (a, b), [P, PACK, PASS], F32)
                nc.sync.dma_start(
                    w1_raw[a, b][:],
                    w1[a * PASS : (a + 1) * PASS, b * PASS : (b + 1) * PASS].rearrange("(p j) c -> p j c", j=PACK),
                )
        nc.sync.dma_start(th_rows[: S2 // P, :], th.rearrange("(c p) -> c p", p=P))
        make_identity(nc, ident[:])

        def half2(h):
            return idx2[:, 32 * h : 32 * (h + 1)]

        v_s = [v_s01, v_s1]
        v_w = [gather("v_w%d" % a, tab_w[a][:].bitcast(U32), idx[:], U32) for a in range(PASSES)]

        h2_w, h2_s = [], []
        for b in range(PASSES):
            grouped = held("h2_g%d" % b, [P, S * PACK], BF16)
            for pair in range(2):
                turned = []
                for jt in (2 * pair, 2 * pair + 1):
                    acc = psum.tile([P, BANK], F32, name="right" if (b, pair) == (1, 0) else "left")
                    for a in range(PASSES):
                        nc.tensor.matmul_mx(
                            out=acc[:],
                            lhsT=v_w[a][:, jt * P : (jt + 1) * P].bitcast(FP8X4),
                            lhsT_scale=v_s[a][:, jt * P : (jt + 1) * P],
                            rhs=w4_w[a][:, 2 * b * PASS : 2 * (b + 1) * PASS].bitcast(FP4X4),
                            rhs_scale=w4_s[:, a * K + b * PASS : a * K + (b + 1) * PASS],
                            start=(a == 0),
                            stop=(a == PASSES - 1),
                        )
                    h2t = ring.tile([P, BANK], BF16, name="h2t")
                    nc.scalar.activation(
                        h2t[:].rearrange("j (u p e) -> j u p e", u=2, e=2),
                        acc[:].rearrange("j (p u e) -> j u p e", u=2, e=2),
                        ACT.Relu,
                    )
                    turned.append(h2t)
                back = psum.tile([P, BANK], F32, name="right")
                for i in range(2):
                    for u in range(2):
                        nc.tensor.transpose(
                            back[:, (2 * i + u) * P : (2 * i + u + 1) * P],
                            turned[i][:].bitcast(F32)[:, u * P : (u + 1) * P],
                            ident[:],
                        )
                nc.scalar.copy(
                    grouped[:].bitcast(F32)[:, pair * BANK : (pair + 1) * BANK].rearrange("p (i j u) -> p i j u", i=2, u=2),
                    back[:].rearrange("p (i u j) -> p i j u", i=2, u=2),
                )
            codes = held("h2_w%d" % b, [P, S], U32)
            plane = held("h2_s%d" % b, [P, S], U8)
            nc.vector.quantize_mx(out=codes[:].bitcast(FP8X4), scales=plane[:], in_=grouped[:])
            h2_w.append(codes)
            h2_s.append(plane)

        v2_s, v2_w = {}, {}

        def gather2_scales(h, tag=None):
            v2_s[h] = gather("v2_s%d" % h, tab_s01[:], half2(h), U8, tag)

        def gather2_words(h, a, tag=None):
            v2_w[h, a] = gather("v2_w%d%d" % (h, a), tab_w[a][:].bitcast(U32), half2(h), U32, tag)

        w1_g, w1_q = {}, {}

        def round_w1(a, b):
            w1_g[a, b] = held("w1_g%d%d" % (a, b), [P, PASS * PACK], BF16)
            dst = w1_g[a, b][:].rearrange("p (t m j) -> p m t j", t=PACK, j=PACK)
            src = w1_raw[a, b][:].rearrange("p j (m t) -> p m t j", t=PACK)
            if (a, b) == ON_SCALAR:
                for half in (slice(0, P // 2), slice(P // 2, P)):
                    nc.scalar.copy(dst[:, half], src[:, half])
            else:
                nc.vector.tensor_copy(dst, src)

        def quantise_w1(a, b):
            codes = held("w1_w%d%d" % (a, b), [P, PASS], U32)
            plane = held("w1_s%d%d" % (a, b), [P, PASS], U8)
            nc.vector.quantize_mx(out=codes[:].bitcast(FP8X4), scales=plane[:], in_=w1_g[a, b][:])
            w1_q[a, b] = codes, plane

        h1_w, h1_s = [], []

        def make_h1(b):
            codes = held("h1_w%d" % b, [P, S], U32)
            plane = held("h1_s%d" % b, [P, S], U8)
            banks = [psum.tile([P, BANK], F32, name="left") for jt in range(S // P)]
            for jt in range(S // P):
                for a in range(PASSES):
                    for t in range(PACK):
                        nc.tensor.matmul_mx(
                            out=banks[jt][:, t * P : (t + 1) * P],
                            lhsT=w1_q[a, b][0][:, t * P : (t + 1) * P].bitcast(FP8X4),
                            lhsT_scale=w1_q[a, b][1][:, t * P : (t + 1) * P],
                            rhs=v_w[a][:, jt * P : (jt + 1) * P].bitcast(FP8X4),
                            rhs_scale=v_s[a][:, jt * P : (jt + 1) * P],
                            start=(a == 0 and t == 0),
                            stop=(a == PASSES - 1 and t == PACK - 1),
                        )
            for pair in range(2):
                grouped = held("h1_g%d%d" % (b, pair), [P, 2 * BANK], BF16)
                for i in range(2):
                    nc.scalar.activation(
                        grouped[:, i * BANK : (i + 1) * BANK].rearrange("p (n t) -> p n t", t=PACK),
                        banks[2 * pair + i][:].rearrange("p (t n) -> p n t", t=PACK),
                        ACT.Abs,
                    )
                cols = slice(2 * pair * P, 2 * (pair + 1) * P)
                nc.vector.quantize_mx(out=codes[:, cols].bitcast(FP8X4), scales=plane[:, cols], in_=grouped[:])
            h1_w.append(codes)
            h1_s.append(plane)

        def match(mt, h_w, h_s, side, notes=slice(0, S)):
            h, cols = mt // 4, slice((mt % 4) * P, (mt % 4 + 1) * P)
            acc = psum.tile([P, BANK], F32, name=side)
            for a in range(PASSES):
                nc.tensor.matmul_mx(
                    out=acc[:, notes],
                    lhsT=v2_w[h, a][:, cols].bitcast(FP8X4),
                    lhsT_scale=v2_s[h][4 * a : P, cols],
                    rhs=h_w[a][:, notes].bitcast(FP8X4),
                    rhs_scale=h_s[a][:, notes],
                    start=(a == 0),
                    stop=(a == PASSES - 1),
                )
            return acc

        e2_less = {}

        def drain_e2(mt, acc):
            e2_less[mt] = held("e2_less%d" % mt, [P, S], F32)
            nc.scalar.activation(e2_less[mt][:], acc[:], ACT.Identity, bias=neg_th[:, mt : mt + 1])

        th_bank = psum.tile([P, BANK], F32, name="right")
        nc.tensor.transpose(th_bank[:, :P], th_rows[:], ident[:])
        nc.scalar.activation(neg_th[:], th_bank[:, : S2 // P], ACT.Identity, scale=-1.0)
        def make_out(mt, notes=slice(0, S)):
            acc = match(mt, h1_w, h1_s, "left", notes)
            result = held("result%d_%d" % (mt, notes.start), [P, S], F32)
            nc.vector.scalar_tensor_tensor(
                result[:, notes], acc[:, notes], neg_th[:, mt : mt + 1], e2_less[mt][:, notes], ALU.add, ALU.min
            )
            nc.sync.dma_start(out[mt * P : (mt + 1) * P, notes], result[:, notes])

        gather2_scales(0)
        gather2_words(0, 0)
        gather2_words(0, 1)
        for a in range(PASSES):
            round_w1(a, 0)
            quantise_w1(a, 0)
        round_w1(0, 1)
        quantise_w1(0, 1)
        round_w1(1, 1)
        make_h1(0)
        e2 = [match(mt, h2_w, h2_s, "right") for mt in range(4)]
        quantise_w1(1, 1)
        make_h1(1)
        gather2_scales(1, "w1_g01")
        gather2_words(1, 0, "h2_g1")
        gather2_words(1, 1, "w1_g11")
        for mt in range(8):
            drain_e2(mt, e2[mt])
            if mt < 4:
                e2.append(match(mt + 4, h2_w, h2_s, "right"))
            if mt < 7:
                make_out(mt)
        make_out(7, slice(0, S // 2))
        make_out(7, slice(S // 2, S))
